import numpy as np
import ml_dtypes


def mxq(x, axis, fmt="e4m3"):
    dtype, down = {"e4m3": (ml_dtypes.float8_e4m3fn, 7), "e5m2": (ml_dtypes.float8_e5m2, 14)}[fmt]
    v = np.moveaxis(np.asarray(x, np.float32).astype(ml_dtypes.bfloat16).astype(np.float64), axis, -1)
    blocks = v.reshape(v.shape[:-1] + (-1, 32))
    amax = np.abs(blocks).max(-1, keepdims=True)
    byte = np.maximum(np.where(amax > 0, np.frexp(amax)[1] - 1 + 127, 0) - down, 1)
    scale = np.exp2(byte - 127.0)
    codes = (blocks / scale).astype(np.float32).astype(dtype).astype(np.float64)
    return np.moveaxis((codes * scale).reshape(v.shape), -1, axis)


WIDE = False


def mx_kscale(k):
    if not WIDE:
        return np.ones(k)
    levels = np.array([10, -10, 5, -5, 0])
    if k % 512:
        return np.exp2(np.random.permutation(np.resize(levels, k // 32))).repeat(32)
    a = np.empty((k // 512, 16))
    for p in range(k // 512):
        a[p, :8] = np.random.permutation(np.resize(levels, 8))
        for g in range(8):
            far = levels[np.abs(levels - a[p, g]) >= 10]
            a[p, g + 8] = far[np.random.randint(len(far))]
    return np.exp2(a.ravel()).repeat(32)


def f64(x):
    return np.asarray(x).astype(np.float64)


def striped(idx):
    return np.tile(np.asarray(idx).reshape(-1, 16).T, (8, 1)).astype(np.uint16)


def unstriped(offs):
    return offs[:16].T.reshape(-1).astype(np.int64)


O, G, K, T, D, M = 9, 256, 4, 2048, 512, 128


def setup_inputs():
    n = np.random.standard_normal
    s = mx_kscale(D)[:, None]
    grid = lambda x: np.round(x * 32) / 32
    part = np.random.randint(1, 128 // K, (O, G, K)) / 64.0
    return {
        "xT": (grid(n((D, T))) * s).astype(np.float32),
        "w": (n((O, D, M)) / np.sqrt(O * D) / s).astype(np.float32),
        "part": np.tile(part.reshape(-1), (128, 1)).astype(np.float32),
        "offs": striped(np.random.randint(0, T, O * G * K)),
    }


def reference(xT, w, part, offs):
    x = f64(xT)[:, unstriped(offs)] * f64(part)[:1]
    e = mxq(x.reshape(D, O, G, K).sum(-1), 0, "e4m3")
    wq = mxq(f64(w), 1, "e4m3")
    y = sum(wq[o].T @ e[:, o] for o in range(O))
    return y

@@ -1,0 +1,163 @@
+from contextlib import ExitStack
+
+import concourse.mybir as mybir
+from concourse.masks import make_identity
+
+O, G, K, T, D, M = 9, 256, 4, 2048, 512, 128
+P = 128
+PACK = 4
+HALVES = G // P
+
+FLOPS = 2 * O * D * M * G
+BYTES = 4 * D * T + 4 * O * D * M + 4 * O * G * K + 2 * P * (O * G * K // 16) + 4 * M * G
+
+F32 = mybir.dt.float32
+BF16 = mybir.dt.bfloat16
+U32 = mybir.dt.uint32
+U16 = mybir.dt.uint16
+U8 = mybir.dt.uint8
+FP8X4 = mybir.dt.float8_e4m3fn_x4
+COPY = mybir.ActivationFunctionType.Copy
+MULT = mybir.AluOpType.mult
+ADD = mybir.AluOpType.add
+
+CHUNK = 512
+V_TAPS = (0, 1, 3, 4, 6, 7, 8)
+
+
+def tile_attend_deform_kernel(tc, xT, w, part, offs, out):
+    nc = tc.nc
+    with ExitStack() as ctx:
+        held = ctx.enter_context(tc.tile_pool(name="held", bufs=1))
+        ring = ctx.enter_context(tc.tile_pool(name="ring", bufs=4))
+        duo = ctx.enter_context(tc.tile_pool(name="duo", bufs=3))
+        psum = ctx.enter_context(tc.psum_pool(name="psum", bufs=1))
+
+        offsets = held.tile([P, O * G * K // 16], U16)
+        ident = held.tile([P, P], F32)
+        part_rows = held.tile([P, G * K // HALVES], F32)
+        words = [held.tile([P, 2 * T], BF16, name="words%d" % u) for u in range(2)]
+
+        nc.vector.memset(part_rows[:], 0.0)
+        make_identity(nc, ident[:])
+        nc.scalar.dma_start(
+            out=part_rows[0 : O * HALVES, :],
+            in_=part[0:1, :].rearrange("a (b e) -> (a b) e", e=G * K // HALVES),
+        )
+
+        x_rows = xT.rearrange("(p t) c -> p t c", t=PACK)
+        for u in range(2):
+            for c in range(0, T, CHUNK):
+                x32 = held.tile([P, 2, CHUNK], F32, name="x32_%d_%d" % (u, c))
+                nc.sync.dma_start(out=x32[:], in_=x_rows[:, 2 * u : 2 * u + 2, c : c + CHUNK])
+                dst = words[u][:, 2 * c : 2 * (c + CHUNK)].rearrange("p (c e) -> p c e", e=2)
+                src = x32[:].rearrange("p e c -> p c e")
+                if u == 0:
+                    nc.vector.tensor_copy(out=dst, in_=src)
+                else:
+                    nc.scalar.activation(out=dst, in_=src, func=COPY)
+            if u == 0:
+                nc.sync.dma_start(offsets[:], offs)
+
+        part_ps = psum.tile([P, 512], F32, tag="xt", bufs=5)
+        for j in range(K):
+            nc.tensor.transpose(part_ps[:, j * P : (j + 1) * P], part_rows[:, j::K], ident[:])
+        part_col = held.tile([P, K, O * HALVES], F32)
+        nc.scalar.activation(
+            out=part_col[:],
+            in_=part_ps[:].rearrange("p (j b) -> p j b", j=K)[:, :, 0 : O * HALVES],
+            func=COPY,
+        )
+
+        w_rows = w.rearrange("o (p j) m -> p o j m", j=PACK)
+        w_bf = held.tile([P, O * M * PACK], BF16, align_bytes=64)
+        w_codes = held.tile([P, O * M], U32, align_bytes=64)
+        w_scales = held.tile([P, O * M], U8, align_bytes=64)
+        for o0 in range(0, O, 3):
+            w32 = held.tile([P, 3, PACK, M], F32, name="w32_%d" % o0)
+            for o in range(3):
+                nc.sync.dma_start(out=w32[:, o], in_=w_rows[:, o0 + o])
+            nc.scalar.activation(
+                out=w_bf[:, o0 * M * PACK : (o0 + 3) * M * PACK].rearrange("p (o m j) -> p o m j", o=3, j=PACK),
+                in_=w32[:].rearrange("p o j m -> p o m j"),
+                func=COPY,
+            )
+        for a, b in ((0, 512), (512, 1024), (1024, 1152)):
+            nc.vector.quantize_mx(
+                out=w_codes[:, a:b].bitcast(FP8X4),
+                scales=w_scales[:, a:b],
+                in_=w_bf[:, PACK * a : PACK * b],
+            )
+
+        acc = psum.tile([M, G], F32)
+        for o in range(O):
+            cols = slice(o * G * K // 16, (o + 1) * G * K // 16)
+            got = []
+            for u in range(2):
+                picked = ring.tile([P, G * K], U32, name="picked%d" % u)
+                nc.vector.tensor_copy(picked[:], words[u][:].bitcast(U32).indirect(offsets[:, cols]))
+                got.append(picked[:].bitcast(F32))
+            prods = []
+            for j in range(K):
+                bank = psum.tile([P, 512], F32, name="bank", tag="xt", bufs=5)
+                for h in range(HALVES):
+                    for u in range(2):
+                        at = (2 * h + u) * P
+                        nc.tensor.transpose(
+                            bank[:, at : at + P],
+                            got[u][:, h * P * K + j : (h + 1) * P * K : K],
+                            ident[:],
+                        )
+                vals = bank[:].bitcast(BF16)
+                prod = duo.tile([P, HALVES * D], F32, name="prod%d" % j)
+                for h in range(HALVES):
+                    part_h = slice(h * D, (h + 1) * D)
+                    scale = part_col[:, j, HALVES * o + h : HALVES * o + h + 1]
+                    if j == K - 1 and o in V_TAPS:
+                        nc.vector.scalar_tensor_tensor(
+                            out=prod[:, part_h], in0=vals[:, part_h], scalar=scale,
+                            in1=prods[2][:, part_h], op0=MULT, op1=ADD,
+                        )
+                    else:
+                        nc.scalar.activation(out=prod[:, part_h], in_=vals[:, part_h], func=COPY, scale=scale)
+                prods.append(prod)
+            sum01 = duo.tile([P, HALVES * D], F32)
+            nc.gpsimd.tensor_tensor(out=sum01[:], in0=prods[0][:], in1=prods[1][:], op=ADD)
+            if o in V_TAPS:
+                sum23 = prods[3]
+            else:
+                sum23 = duo.tile([P, HALVES * D], F32, name="sum23")
+                nc.gpsimd.tensor_tensor(out=sum23[:], in0=prods[2][:], in1=prods[3][:], op=ADD)
+            e_rows = duo.tile([P, HALVES * D], BF16, align_bytes=64)
+            nc.gpsimd.tensor_tensor(out=e_rows[:], in0=sum01[:], in1=sum23[:], op=ADD)
+
+            e_words = e_rows[:].bitcast(F32)
+            e_ps = psum.tile([P, 512], F32, name="e_ps", tag="e_ps", bufs=2)
+            for h in range(HALVES):
+                for u in range(2):
+                    nc.tensor.transpose(
+                        e_ps[:, u * G + h * P : u * G + (h + 1) * P],
+                        e_words[:, (2 * h + u) * P : (2 * h + u + 1) * P],
+                        ident[:],
+                    )
+            e_k = duo.tile([P, G * PACK], BF16, align_bytes=64)
+            nc.scalar.copy(
+                out=e_k[:].bitcast(F32).rearrange("p (g u) -> p g u", u=2),
+                in_=e_ps[:].rearrange("p (u g) -> p g u", u=2),
+            )
+            e_codes = duo.tile([P, G], U32, align_bytes=64)
+            e_scales = duo.tile([P, G], U8, align_bytes=64)
+            nc.vector.quantize_mx(out=e_codes[:].bitcast(FP8X4), scales=e_scales[:], in_=e_k[:])
+            m_cols = slice(o * M, (o + 1) * M)
+            nc.tensor.matmul_mx(
+                out=acc[:],
+                lhsT=w_codes[:, m_cols].bitcast(FP8X4),
+                lhsT_scale=w_scales[:, m_cols],
+                rhs=e_codes[:].bitcast(FP8X4),
+                rhs_scale=e_scales[:],
+                start=(o == 0),
+                stop=(o == O - 1),
+            )
+        result = held.tile([M, G], F32)
+        nc.vector.tensor_copy(out=result[:], in_=acc[:])
+        nc.sync.dma_start(out=out, in_=result[:])

@@ -7,6 +7,7 @@ O, G, K, T, D, M = 9, 256, 4, 2048, 512, 128
 P = 128
 PACK = 4
 HALVES = G // P
+W = D // HALVES
 
 FLOPS = 2 * O * D * M * G
 BYTES = 4 * D * T + 4 * O * D * M + 4 * O * G * K + 2 * P * (O * G * K // 16) + 4 * M * G
@@ -22,15 +23,16 @@ MULT = mybir.AluOpType.mult
 ADD = mybir.AluOpType.add
 
 CHUNK = 512
-V_TAPS = (0, 1, 3, 4, 6, 7, 8)
+V_CORNERS = (0, 2, 1, 2, 1, 2, 1, 2, 0)
+W_AT = {2: 0, 3: 1, 4: 2}
+MM_AT = (5, 7, 8)
 
 
 def tile_attend_deform_kernel(tc, xT, w, part, offs, out):
     nc = tc.nc
     with ExitStack() as ctx:
         held = ctx.enter_context(tc.tile_pool(name="held", bufs=1))
-        ring = ctx.enter_context(tc.tile_pool(name="ring", bufs=4))
-        duo = ctx.enter_context(tc.tile_pool(name="duo", bufs=3))
+        duo = ctx.enter_context(tc.tile_pool(name="duo", bufs=2))
         psum = ctx.enter_context(tc.psum_pool(name="psum", bufs=1))
 
         offsets = held.tile([P, O * G * K // 16], U16)
@@ -52,7 +54,7 @@ def tile_attend_deform_kernel(tc, xT, w, part, offs, out):
                 nc.sync.dma_start(out=x32[:], in_=x_rows[:, 2 * u : 2 * u + 2, c : c + CHUNK])
                 dst = words[u][:, 2 * c : 2 * (c + CHUNK)].rearrange("p (c e) -> p c e", e=2)
                 src = x32[:].rearrange("p e c -> p c e")
-                if u == 0:
+                if u == 0 or c + CHUNK == T:
                     nc.vector.tensor_copy(out=dst, in_=src)
                 else:
                     nc.scalar.activation(out=dst, in_=src, func=COPY)
@@ -73,91 +75,169 @@ def tile_attend_deform_kernel(tc, xT, w, part, offs, out):
         w_bf = held.tile([P, O * M * PACK], BF16, align_bytes=64)
         w_codes = held.tile([P, O * M], U32, align_bytes=64)
         w_scales = held.tile([P, O * M], U8, align_bytes=64)
+        w_raw = []
         for o0 in range(0, O, 3):
             w32 = held.tile([P, 3, PACK, M], F32, name="w32_%d" % o0)
             for o in range(3):
                 nc.sync.dma_start(out=w32[:, o], in_=w_rows[:, o0 + o])
+            w_raw.append(w32)
+
+        def quantise_w(third):
+            a, b = third * 3 * M, (third + 1) * 3 * M
             nc.scalar.activation(
-                out=w_bf[:, o0 * M * PACK : (o0 + 3) * M * PACK].rearrange("p (o m j) -> p o m j", o=3, j=PACK),
-                in_=w32[:].rearrange("p o j m -> p o m j"),
+                out=w_bf[:, a * PACK : b * PACK].rearrange("p (o m j) -> p o m j", o=3, j=PACK),
+                in_=w_raw[third][:].rearrange("p o j m -> p o m j"),
                 func=COPY,
             )
-        for a, b in ((0, 512), (512, 1024), (1024, 1152)):
-            nc.vector.quantize_mx(
-                out=w_codes[:, a:b].bitcast(FP8X4),
-                scales=w_scales[:, a:b],
-                in_=w_bf[:, PACK * a : PACK * b],
-            )
+            for c in range(a, b, M):
+                nc.vector.quantize_mx(
+                    out=w_codes[:, c : c + M].bitcast(FP8X4),
+                    scales=w_scales[:, c : c + M],
+                    in_=w_bf[:, PACK * c : PACK * (c + M)],
+                )
 
         acc = psum.tile([M, G], F32)
-        for o in range(O):
-            cols = slice(o * G * K // 16, (o + 1) * G * K // 16)
-            got = []
-            for u in range(2):
-                picked = ring.tile([P, G * K], U32, name="picked%d" % u)
-                nc.vector.tensor_copy(picked[:], words[u][:].bitcast(U32).indirect(offsets[:, cols]))
-                got.append(picked[:].bitcast(F32))
-            prods = []
-            for j in range(K):
-                bank = psum.tile([P, 512], F32, name="bank", tag="xt", bufs=5)
-                for h in range(HALVES):
-                    for u in range(2):
-                        at = (2 * h + u) * P
-                        nc.tensor.transpose(
-                            bank[:, at : at + P],
-                            got[u][:, h * P * K + j : (h + 1) * P * K : K],
-                            ident[:],
-                        )
-                vals = bank[:].bitcast(BF16)
-                prod = duo.tile([P, HALVES * D], F32, name="prod%d" % j)
-                for h in range(HALVES):
-                    part_h = slice(h * D, (h + 1) * D)
-                    scale = part_col[:, j, HALVES * o + h : HALVES * o + h + 1]
-                    if j == K - 1 and o in V_TAPS:
-                        nc.vector.scalar_tensor_tensor(
-                            out=prod[:, part_h], in0=vals[:, part_h], scalar=scale,
-                            in1=prods[2][:, part_h], op0=MULT, op1=ADD,
-                        )
-                    else:
-                        nc.scalar.activation(out=prod[:, part_h], in_=vals[:, part_h], func=COPY, scale=scale)
-                prods.append(prod)
-            sum01 = duo.tile([P, HALVES * D], F32)
-            nc.gpsimd.tensor_tensor(out=sum01[:], in0=prods[0][:], in1=prods[1][:], op=ADD)
-            if o in V_TAPS:
-                sum23 = prods[3]
-            else:
-                sum23 = duo.tile([P, HALVES * D], F32, name="sum23")
-                nc.gpsimd.tensor_tensor(out=sum23[:], in0=prods[2][:], in1=prods[3][:], op=ADD)
-            e_rows = duo.tile([P, HALVES * D], BF16, align_bytes=64)
-            nc.gpsimd.tensor_tensor(out=e_rows[:], in0=sum01[:], in1=sum23[:], op=ADD)
+        e_codes = [held.tile([P, G], U32, name="e_codes%d" % o, align_bytes=64) for o in range(O)]
+        e_scales = [held.tile([P, G], U8, name="e_scales%d" % o, align_bytes=64) for o in range(O)]
 
-            e_words = e_rows[:].bitcast(F32)
+        def gather(picked, u, o, a, b):
+            cols = slice((o * G * K + a) // 16, (o * G * K + b) // 16)
+            nc.vector.tensor_copy(picked[:, a:b], words[u][:].bitcast(U32).indirect(offsets[:, cols]))
+
+        def turn(picked, pieces):
+            bank = psum.tile([P, 512], F32, name="bank", tag="xt", bufs=5)
+            for i in range(len(pieces)):
+                u, h, j = pieces[i]
+                entries = picked[u][:].bitcast(F32)[:, h * P * K + j : (h + 1) * P * K : K]
+                nc.tensor.transpose(bank[:, i * P : (i + 1) * P], entries, ident[:])
+            return bank[:].bitcast(BF16)
+
+        def scale(o, h, j):
+            return part_col[:, j, HALVES * o + h : HALVES * o + h + 1]
+
+        def turn_back(e_rows, halves, e_k):
+            e_words = e_rows.bitcast(F32)
+            n = len(halves) * P
             e_ps = psum.tile([P, 512], F32, name="e_ps", tag="e_ps", bufs=2)
-            for h in range(HALVES):
+            for i in range(len(halves)):
                 for u in range(2):
                     nc.tensor.transpose(
-                        e_ps[:, u * G + h * P : u * G + (h + 1) * P],
-                        e_words[:, (2 * h + u) * P : (2 * h + u + 1) * P],
+                        e_ps[:, u * n + i * P : u * n + (i + 1) * P],
+                        e_words[:, (2 * i + u) * P : (2 * i + u + 1) * P],
                         ident[:],
                     )
-            e_k = duo.tile([P, G * PACK], BF16, align_bytes=64)
             nc.scalar.copy(
-                out=e_k[:].bitcast(F32).rearrange("p (g u) -> p g u", u=2),
-                in_=e_ps[:].rearrange("p (u g) -> p g u", u=2),
+                out=e_k.bitcast(F32).rearrange("p (g u) -> p g u", u=2),
+                in_=e_ps[:, 0 : 2 * n].rearrange("p (u g) -> p g u", u=2),
             )
-            e_codes = duo.tile([P, G], U32, align_bytes=64)
-            e_scales = duo.tile([P, G], U8, align_bytes=64)
-            nc.vector.quantize_mx(out=e_codes[:].bitcast(FP8X4), scales=e_scales[:], in_=e_k[:])
-            m_cols = slice(o * M, (o + 1) * M)
-            nc.tensor.matmul_mx(
-                out=acc[:],
-                lhsT=w_codes[:, m_cols].bitcast(FP8X4),
-                lhsT_scale=w_scales[:, m_cols],
-                rhs=e_codes[:].bitcast(FP8X4),
-                rhs_scale=e_scales[:],
-                start=(o == 0),
-                stop=(o == O - 1),
+
+        def quantise_e(o, e_k, a, b):
+            nc.vector.quantize_mx(
+                out=e_codes[o][:, a:b].bitcast(FP8X4), scales=e_scales[o][:, a:b], in_=e_k[:, PACK * a : PACK * b]
             )
+
+        done = 0
+        for o in range(O):
+            e_k = duo.tile([P, G * PACK], BF16, align_bytes=64)
+            picked = [duo.tile([P, G * K], U32, name="picked%d" % u) for u in range(2)]
+            if o == 0:
+                e_rows = duo.tile([P, HALVES, 2, W], BF16, align_bytes=64)
+                for u in range(2):
+                    gather(picked[u], u, o, 0, G * K)
+                    prods = held.tile([P, K, HALVES * W], F32, name="first%d" % u)
+                    for j0 in range(0, K, 2):
+                        vals = turn(picked, [(u, h, j) for j in (j0, j0 + 1) for h in range(HALVES)])
+                        for i in range(4):
+                            j, h = j0 + i // 2, i % 2
+                            nc.scalar.activation(
+                                out=prods[:, j, h * W : (h + 1) * W], in_=vals[:, i * W : (i + 1) * W],
+                                func=COPY, scale=scale(o, h, j),
+                            )
+                    pairs = held.tile([P, 2, HALVES * W], F32, name="pairs%d" % u)
+                    nc.gpsimd.tensor_tensor(out=pairs[:], in0=prods[:, 0:2], in1=prods[:, 2:4], op=ADD)
+                    nc.gpsimd.tensor_tensor(
+                        out=e_rows[:, :, u], in0=pairs[:, 0].rearrange("p (h w) -> p h w", h=HALVES),
+                        in1=pairs[:, 1].rearrange("p (h w) -> p h w", h=HALVES), op=ADD,
+                    )
+                turn_back(e_rows[:].rearrange("p h u w -> p (h u w)"), (0, 1), e_k[:])
+                quantise_e(o, e_k, 0, G)
+            elif o < O - 1:
+                for u in range(2):
+                    gather(picked[u], u, o, 0, G * K)
+                prods = []
+                for j in range(K):
+                    vals = turn(picked, [(u, h, j) for h in range(HALVES) for u in range(2)])
+                    prod = duo.tile([P, HALVES * D], F32, name="prod%d" % j)
+                    for h in range(HALVES):
+                        part_h = slice(h * D, (h + 1) * D)
+                        if j >= K - V_CORNERS[o]:
+                            onto = prods[2] if V_CORNERS[o] == 1 else prods[j - 2]
+                            nc.vector.scalar_tensor_tensor(
+                                out=prod[:, part_h], in0=vals[:, part_h], scalar=scale(o, h, j),
+                                in1=onto[:, part_h], op0=MULT, op1=ADD,
+                            )
+                        else:
+                            nc.scalar.activation(
+                                out=prod[:, part_h], in_=vals[:, part_h], func=COPY, scale=scale(o, h, j)
+                            )
+                    prods.append(prod)
+                if V_CORNERS[o] == 2:
+                    halves = (prods[2], prods[3])
+                else:
+                    sum01 = duo.tile([P, HALVES * D], F32)
+                    nc.gpsimd.tensor_tensor(out=sum01[:], in0=prods[0][:], in1=prods[1][:], op=ADD)
+                    halves = (sum01, prods[3])
+                    if V_CORNERS[o] == 0:
+                        sum23 = duo.tile([P, HALVES * D], F32)
+                        nc.gpsimd.tensor_tensor(out=sum23[:], in0=prods[2][:], in1=prods[3][:], op=ADD)
+                        halves = (sum01, sum23)
+                e_rows = duo.tile([P, HALVES * D], BF16, align_bytes=64)
+                nc.gpsimd.tensor_tensor(out=e_rows[:], in0=halves[0][:], in1=halves[1][:], op=ADD)
+                turn_back(e_rows[:], (0, 1), e_k[:])
+                quantise_e(o, e_k, 0, G)
+            else:
+                for h in range(HALVES):
+                    for u in range(2):
+                        gather(picked[u], u, o, h * P * K, (h + 1) * P * K)
+                    last = h == HALVES - 1
+                    e_rows = duo.tile([P, D], BF16, name="e_last", align_bytes=64)
+                    vals = {}
+                    for js in ((0,), (1, 2), (3,)) if last else ((0, 1), (2, 3)):
+                        bank = turn(picked, [(u, h, j) for j in js for u in range(2)])
+                        for i in range(len(js)):
+                            vals[js[i]] = bank[:, i * D : (i + 1) * D]
+                    if last:
+                        run = held.tile([P, 3, D], F32)
+                        nc.scalar.activation(out=run[:, 0], in_=vals[0], func=COPY, scale=scale(o, h, 0))
+                        for j in range(1, K):
+                            nc.vector.scalar_tensor_tensor(
+                                out=e_rows[:] if j == K - 1 else run[:, j], in0=vals[j], scalar=scale(o, h, j),
+                                in1=run[:, j - 1], op0=MULT, op1=ADD,
+                            )
+                    else:
+                        prods = held.tile([P, K, D], F32, name="last")
+                        pairs = held.tile([P, 2, D], F32, name="last_pairs")
+                        for j in range(K):
+                            nc.scalar.activation(out=prods[:, j], in_=vals[j], func=COPY, scale=scale(o, h, j))
+                        nc.gpsimd.tensor_tensor(out=pairs[:], in0=prods[:, 0:2], in1=prods[:, 2:4], op=ADD)
+                        nc.gpsimd.tensor_tensor(out=e_rows[:], in0=pairs[:, 0], in1=pairs[:, 1], op=ADD)
+                    turn_back(e_rows[:], (h,), e_k[:, h * P * PACK : (h + 1) * P * PACK])
+                    quantise_e(o, e_k, h * P, (h + 1) * P)
+            if o in W_AT:
+                quantise_w(W_AT[o])
+            if o in MM_AT:
+                for q in range(done, o + 1):
+                    m_cols = slice(q * M, (q + 1) * M)
+                    nc.tensor.matmul_mx(
+                        out=acc[:],
+                        lhsT=w_codes[:, m_cols].bitcast(FP8X4),
+                        lhsT_scale=w_scales[:, m_cols],
+                        rhs=e_codes[q][:].bitcast(FP8X4),
+                        rhs_scale=e_scales[q][:],
+                        start=(q == 0),
+                        stop=(q == O - 1),
+                    )
+                done = o + 1
         result = held.tile([M, G], F32)
         nc.vector.tensor_copy(out=result[:], in_=acc[:])
         nc.sync.dma_start(out=out, in_=result[:])

@@ -22,10 +22,17 @@ COPY = mybir.ActivationFunctionType.Copy
 MULT = mybir.AluOpType.mult
 ADD = mybir.AluOpType.add
 
-CHUNK = 512
-V_CORNERS = (0, 2, 1, 2, 1, 2, 1, 2, 0)
-W_AT = {2: 0, 3: 1, 4: 2}
+CHUNKS = ((0, 512), (512, 512), (1024, 512), (1536, 256), (1792, 256))
+V_CORNERS = (0, 1, 1, 1, 1, 0, 1, 2, 0)
+W_AT = ((1, 0, 4, "G"), (2, 4, 8, "S"), (3, 8, 9, "S"))
 MM_AT = (5, 7, 8)
+U1_ON_V = ()
+V_ADDS = (7,)
+TAIL = ("chain", "pairs")
+PICK_BUFS = 2
+PROD_BUFS = 3
+XT = 5
+EP = 2
 
 
 def tile_attend_deform_kernel(tc, xT, w, part, offs, out):
@@ -49,19 +56,19 @@ def tile_attend_deform_kernel(tc, xT, w, part, offs, out):
 
         x_rows = xT.rearrange("(p t) c -> p t c", t=PACK)
         for u in range(2):
-            for c in range(0, T, CHUNK):
-                x32 = held.tile([P, 2, CHUNK], F32, name="x32_%d_%d" % (u, c))
-                nc.sync.dma_start(out=x32[:], in_=x_rows[:, 2 * u : 2 * u + 2, c : c + CHUNK])
-                dst = words[u][:, 2 * c : 2 * (c + CHUNK)].rearrange("p (c e) -> p c e", e=2)
+            for c, wide in CHUNKS:
+                x32 = held.tile([P, 2, wide], F32, name="x32_%d_%d" % (u, c))
+                nc.sync.dma_start(out=x32[:], in_=x_rows[:, 2 * u : 2 * u + 2, c : c + wide])
+                dst = words[u][:, 2 * c : 2 * (c + wide)].rearrange("p (c e) -> p c e", e=2)
                 src = x32[:].rearrange("p e c -> p c e")
-                if u == 0 or c + CHUNK == T:
+                if u == 0 or c in U1_ON_V:
                     nc.vector.tensor_copy(out=dst, in_=src)
                 else:
                     nc.scalar.activation(out=dst, in_=src, func=COPY)
             if u == 0:
                 nc.sync.dma_start(offsets[:], offs)
 
-        part_ps = psum.tile([P, 512], F32, tag="xt", bufs=5)
+        part_ps = psum.tile([P, 512], F32, tag="xt", bufs=XT)
         for j in range(K):
             nc.tensor.transpose(part_ps[:, j * P : (j + 1) * P], part_rows[:, j::K], ident[:])
         part_col = held.tile([P, K, O * HALVES], F32)
@@ -75,26 +82,24 @@ def tile_attend_deform_kernel(tc, xT, w, part, offs, out):
         w_bf = held.tile([P, O * M * PACK], BF16, align_bytes=64)
         w_codes = held.tile([P, O * M], U32, align_bytes=64)
         w_scales = held.tile([P, O * M], U8, align_bytes=64)
-        w_raw = []
-        for o0 in range(0, O, 3):
-            w32 = held.tile([P, 3, PACK, M], F32, name="w32_%d" % o0)
-            for o in range(3):
-                nc.sync.dma_start(out=w32[:, o], in_=w_rows[:, o0 + o])
-            w_raw.append(w32)
 
-        def quantise_w(third):
-            a, b = third * 3 * M, (third + 1) * 3 * M
-            nc.scalar.activation(
-                out=w_bf[:, a * PACK : b * PACK].rearrange("p (o m j) -> p o m j", o=3, j=PACK),
-                in_=w_raw[third][:].rearrange("p o j m -> p o m j"),
-                func=COPY,
+        def prepare_w(a, b, engine):
+            w32 = held.tile([P, 4, PACK, M], F32, name="first1")
+            for o in range(a, b):
+                nc.sync.dma_start(out=w32[:, o - a], in_=w_rows[:, o])
+            dst = w_bf[:, a * M * PACK : b * M * PACK].rearrange("p (o m j) -> p o m j", o=b - a, j=PACK)
+            src = w32[:, 0 : b - a].rearrange("p o j m -> p o m j")
+            if engine == "V":
+                nc.vector.tensor_copy(out=dst, in_=src)
+            elif engine == "G":
+                nc.gpsimd.tensor_scalar(out=dst, in0=src, scalar1=1.0, scalar2=0.0, op0=MULT, op1=ADD)
+            else:
+                nc.scalar.activation(out=dst, in_=src, func=COPY)
+            nc.vector.quantize_mx(
+                out=w_codes[:, a * M : b * M].bitcast(FP8X4),
+                scales=w_scales[:, a * M : b * M],
+                in_=w_bf[:, PACK * a * M : PACK * b * M],
             )
-            for c in range(a, b, M):
-                nc.vector.quantize_mx(
-                    out=w_codes[:, c : c + M].bitcast(FP8X4),
-                    scales=w_scales[:, c : c + M],
-                    in_=w_bf[:, PACK * c : PACK * (c + M)],
-                )
 
         acc = psum.tile([M, G], F32)
         e_codes = [held.tile([P, G], U32, name="e_codes%d" % o, align_bytes=64) for o in range(O)]
@@ -105,7 +110,7 @@ def tile_attend_deform_kernel(tc, xT, w, part, offs, out):
             nc.vector.tensor_copy(picked[:, a:b], words[u][:].bitcast(U32).indirect(offsets[:, cols]))
 
         def turn(picked, pieces):
-            bank = psum.tile([P, 512], F32, name="bank", tag="xt", bufs=5)
+            bank = psum.tile([P, 512], F32, name="bank", tag="xt", bufs=XT)
             for i in range(len(pieces)):
                 u, h, j = pieces[i]
                 entries = picked[u][:].bitcast(F32)[:, h * P * K + j : (h + 1) * P * K : K]
@@ -118,7 +123,7 @@ def tile_attend_deform_kernel(tc, xT, w, part, offs, out):
         def turn_back(e_rows, halves, e_k):
             e_words = e_rows.bitcast(F32)
             n = len(halves) * P
-            e_ps = psum.tile([P, 512], F32, name="e_ps", tag="e_ps", bufs=2)
+            e_ps = psum.tile([P, 512], F32, name="e_ps", tag="e_ps", bufs=EP)
             for i in range(len(halves)):
                 for u in range(2):
                     nc.tensor.transpose(
@@ -139,7 +144,7 @@ def tile_attend_deform_kernel(tc, xT, w, part, offs, out):
         done = 0
         for o in range(O):
             e_k = duo.tile([P, G * PACK], BF16, align_bytes=64)
-            picked = [duo.tile([P, G * K], U32, name="picked%d" % u) for u in range(2)]
+            picked = [duo.tile([P, G * K], U32, name="picked%d" % u, bufs=PICK_BUFS) for u in range(2)]
             if o == 0:
                 e_rows = duo.tile([P, HALVES, 2, W], BF16, align_bytes=64)
                 for u in range(2):
@@ -167,7 +172,7 @@ def tile_attend_deform_kernel(tc, xT, w, part, offs, out):
                 prods = []
                 for j in range(K):
                     vals = turn(picked, [(u, h, j) for h in range(HALVES) for u in range(2)])
-                    prod = duo.tile([P, HALVES * D], F32, name="prod%d" % j)
+                    prod = duo.tile([P, HALVES * D], F32, name="prod%d" % j, bufs=PROD_BUFS)
                     for h in range(HALVES):
                         part_h = slice(h * D, (h + 1) * D)
                         if j >= K - V_CORNERS[o]:
@@ -192,39 +197,42 @@ def tile_attend_deform_kernel(tc, xT, w, part, offs, out):
                         nc.gpsimd.tensor_tensor(out=sum23[:], in0=prods[2][:], in1=prods[3][:], op=ADD)
                         halves = (sum01, sum23)
                 e_rows = duo.tile([P, HALVES * D], BF16, align_bytes=64)
-                nc.gpsimd.tensor_tensor(out=e_rows[:], in0=halves[0][:], in1=halves[1][:], op=ADD)
+                adder = nc.vector if o in V_ADDS else nc.gpsimd
+                adder.tensor_tensor(out=e_rows[:], in0=halves[0][:], in1=halves[1][:], op=ADD)
                 turn_back(e_rows[:], (0, 1), e_k[:])
                 quantise_e(o, e_k, 0, G)
             else:
                 for h in range(HALVES):
                     for u in range(2):
                         gather(picked[u], u, o, h * P * K, (h + 1) * P * K)
-                    last = h == HALVES - 1
+                    kind = TAIL[h]
                     e_rows = duo.tile([P, D], BF16, name="e_last", align_bytes=64)
                     vals = {}
-                    for js in ((0,), (1, 2), (3,)) if last else ((0, 1), (2, 3)):
+                    for js in ((0,), (1, 2), (3,)) if kind == "chain" else ((0, 1), (2, 3)):
                         bank = turn(picked, [(u, h, j) for j in js for u in range(2)])
                         for i in range(len(js)):
                             vals[js[i]] = bank[:, i * D : (i + 1) * D]
-                    if last:
-                        run = held.tile([P, 3, D], F32)
-                        nc.scalar.activation(out=run[:, 0], in_=vals[0], func=COPY, scale=scale(o, h, 0))
-                        for j in range(1, K):
-                            nc.vector.scalar_tensor_tensor(
-                                out=e_rows[:] if j == K - 1 else run[:, j], in0=vals[j], scalar=scale(o, h, j),
-                                in1=run[:, j - 1], op0=MULT, op1=ADD,
-                            )
-                    else:
-                        prods = held.tile([P, K, D], F32, name="last")
-                        pairs = held.tile([P, 2, D], F32, name="last_pairs")
-                        for j in range(K):
+                    prods = held.tile([P, K, D], F32, name="last%d" % h)
+                    pairs = held.tile([P, 2, D], F32, name="last_pairs%d" % h)
+                    on_scalar = {"chain": 1, "pairs": 2, "scalar": 4}[kind]
+                    for j in range(K):
+                        if j < on_scalar:
                             nc.scalar.activation(out=prods[:, j], in_=vals[j], func=COPY, scale=scale(o, h, j))
+                        else:
+                            nc.vector.scalar_tensor_tensor(
+                                out=e_rows[:] if kind == "chain" and j == K - 1 else prods[:, j], in0=vals[j],
+                                scalar=scale(o, h, j), in1=prods[:, j - on_scalar], op0=MULT, op1=ADD,
+                            )
+                    if kind == "pairs":
+                        nc.vector.tensor_tensor(out=e_rows[:], in0=prods[:, 2], in1=prods[:, 3], op=ADD)
+                    elif kind == "scalar":
                         nc.gpsimd.tensor_tensor(out=pairs[:], in0=prods[:, 0:2], in1=prods[:, 2:4], op=ADD)
                         nc.gpsimd.tensor_tensor(out=e_rows[:], in0=pairs[:, 0], in1=pairs[:, 1], op=ADD)
                     turn_back(e_rows[:], (h,), e_k[:, h * P * PACK : (h + 1) * P * PACK])
                     quantise_e(o, e_k, h * P, (h + 1) * P)
-            if o in W_AT:
-                quantise_w(W_AT[o])
+            for at, a, b, engine in W_AT:
+                if at == o:
+                    prepare_w(a, b, engine)
             if o in MM_AT:
                 for q in range(done, o + 1):
                     m_cols = slice(q * M, (q + 1) * M)

@@ -23,16 +23,17 @@ MULT = mybir.AluOpType.mult
 ADD = mybir.AluOpType.add
 
 CHUNKS = ((0, 512), (512, 512), (1024, 512), (1536, 256), (1792, 256))
-V_CORNERS = (0, 1, 1, 1, 1, 0, 1, 2, 0)
-W_AT = ((1, 0, 4, "G"), (2, 4, 8, "S"), (3, 8, 9, "S"))
-MM_AT = (5, 7, 8)
-U1_ON_V = ()
+V_CORNERS = (0, 1, 1, 1, 1, 2, 0, 2, 0)
+W_AT = ((1, 0, 4, "G"), (2, 4, 8, "S"), (4, 8, 9, "S"))
+MM_AT = (3, 7, 8)
+U1_ON_V = (1792,)
 V_ADDS = (7,)
-TAIL = ("chain", "pairs")
+TAIL = ("pairs", "chain")
 PICK_BUFS = 2
-PROD_BUFS = 3
+PROD_BUFS = 2
 XT = 5
 EP = 2
+E_GROUPS = ((0, 1, 2, 3), (4, 5, 6, 7), (8,))
 
 
 def tile_attend_deform_kernel(tc, xT, w, part, offs, out):
@@ -55,9 +56,11 @@ def tile_attend_deform_kernel(tc, xT, w, part, offs, out):
         )
 
         x_rows = xT.rearrange("(p t) c -> p t c", t=PACK)
+        chunk = 0
         for u in range(2):
             for c, wide in CHUNKS:
-                x32 = held.tile([P, 2, wide], F32, name="x32_%d_%d" % (u, c))
+                x32 = duo.tile([P, 2, wide], F32, name="x32", tag="prod%d" % (chunk % K), bufs=PROD_BUFS)
+                chunk += 1
                 nc.sync.dma_start(out=x32[:], in_=x_rows[:, 2 * u : 2 * u + 2, c : c + wide])
                 dst = words[u][:, 2 * c : 2 * (c + wide)].rearrange("p (c e) -> p c e", e=2)
                 src = x32[:].rearrange("p e c -> p c e")
@@ -102,8 +105,17 @@ def tile_attend_deform_kernel(tc, xT, w, part, offs, out):
             )
 
         acc = psum.tile([M, G], F32)
-        e_codes = [held.tile([P, G], U32, name="e_codes%d" % o, align_bytes=64) for o in range(O)]
-        e_scales = [held.tile([P, G], U8, name="e_scales%d" % o, align_bytes=64) for o in range(O)]
+        e_codes, e_scales, e_vals, closes = {}, {}, {}, {}
+        for group in E_GROUPS:
+            n = len(group)
+            vals = held.tile([P, n * G * PACK], BF16, name="e_vals%d" % group[0], align_bytes=64)
+            codes = held.tile([P, n * G], U32, name="e_codes%d" % group[0], align_bytes=64)
+            scales = held.tile([P, n * G], U8, name="e_scales%d" % group[0], align_bytes=64)
+            for i in range(n):
+                e_vals[group[i]] = vals[:, i * G * PACK : (i + 1) * G * PACK]
+                e_codes[group[i]] = codes[:, i * G : (i + 1) * G]
+                e_scales[group[i]] = scales[:, i * G : (i + 1) * G]
+            closes[group[-1]] = (vals, codes, scales)
 
         def gather(picked, u, o, a, b):
             cols = slice((o * G * K + a) // 16, (o * G * K + b) // 16)
@@ -136,14 +148,12 @@ def tile_attend_deform_kernel(tc, xT, w, part, offs, out):
                 in_=e_ps[:, 0 : 2 * n].rearrange("p (u g) -> p g u", u=2),
             )
 
-        def quantise_e(o, e_k, a, b):
-            nc.vector.quantize_mx(
-                out=e_codes[o][:, a:b].bitcast(FP8X4), scales=e_scales[o][:, a:b], in_=e_k[:, PACK * a : PACK * b]
-            )
+        def quantise_e(vals, codes, scales):
+            nc.vector.quantize_mx(out=codes.bitcast(FP8X4), scales=scales, in_=vals)
 
         done = 0
         for o in range(O):
-            e_k = duo.tile([P, G * PACK], BF16, align_bytes=64)
+            e_k = e_vals[o]
             picked = [duo.tile([P, G * K], U32, name="picked%d" % u, bufs=PICK_BUFS) for u in range(2)]
             if o == 0:
                 e_rows = duo.tile([P, HALVES, 2, W], BF16, align_bytes=64)
@@ -164,8 +174,7 @@ def tile_attend_deform_kernel(tc, xT, w, part, offs, out):
                         out=e_rows[:, :, u], in0=pairs[:, 0].rearrange("p (h w) -> p h w", h=HALVES),
                         in1=pairs[:, 1].rearrange("p (h w) -> p h w", h=HALVES), op=ADD,
                     )
-                turn_back(e_rows[:].rearrange("p h u w -> p (h u w)"), (0, 1), e_k[:])
-                quantise_e(o, e_k, 0, G)
+                turn_back(e_rows[:].rearrange("p h u w -> p (h u w)"), (0, 1), e_k)
             elif o < O - 1:
                 for u in range(2):
                     gather(picked[u], u, o, 0, G * K)
@@ -199,8 +208,7 @@ def tile_attend_deform_kernel(tc, xT, w, part, offs, out):
                 e_rows = duo.tile([P, HALVES * D], BF16, align_bytes=64)
                 adder = nc.vector if o in V_ADDS else nc.gpsimd
                 adder.tensor_tensor(out=e_rows[:], in0=halves[0][:], in1=halves[1][:], op=ADD)
-                turn_back(e_rows[:], (0, 1), e_k[:])
-                quantise_e(o, e_k, 0, G)
+                turn_back(e_rows[:], (0, 1), e_k)
             else:
                 for h in range(HALVES):
                     for u in range(2):
@@ -212,9 +220,8 @@ def tile_attend_deform_kernel(tc, xT, w, part, offs, out):
                         bank = turn(picked, [(u, h, j) for j in js for u in range(2)])
                         for i in range(len(js)):
                             vals[js[i]] = bank[:, i * D : (i + 1) * D]
-                    prods = held.tile([P, K, D], F32, name="last%d" % h)
-                    pairs = held.tile([P, 2, D], F32, name="last_pairs%d" % h)
-                    on_scalar = {"chain": 1, "pairs": 2, "scalar": 4}[kind]
+                    prods = held.tile([P, K, D], F32, name="last%d" % h, tag="first%d" % h)
+                    on_scalar = {"chain": 1, "pairs": 2}[kind]
                     for j in range(K):
                         if j < on_scalar:
                             nc.scalar.activation(out=prods[:, j], in_=vals[j], func=COPY, scale=scale(o, h, j))
@@ -225,11 +232,12 @@ def tile_attend_deform_kernel(tc, xT, w, part, offs, out):
                             )
                     if kind == "pairs":
                         nc.vector.tensor_tensor(out=e_rows[:], in0=prods[:, 2], in1=prods[:, 3], op=ADD)
-                    elif kind == "scalar":
-                        nc.gpsimd.tensor_tensor(out=pairs[:], in0=prods[:, 0:2], in1=prods[:, 2:4], op=ADD)
-                        nc.gpsimd.tensor_tensor(out=e_rows[:], in0=pairs[:, 0], in1=pairs[:, 1], op=ADD)
                     turn_back(e_rows[:], (h,), e_k[:, h * P * PACK : (h + 1) * P * PACK])
-                    quantise_e(o, e_k, h * P, (h + 1) * P)
+                    cols = slice(h * P, (h + 1) * P)
+                    quantise_e(e_k[:, h * P * PACK : (h + 1) * P * PACK], e_codes[o][:, cols], e_scales[o][:, cols])
+            if o in closes and o < O - 1:
+                vals, codes, scales = closes[o]
+                quantise_e(vals[:], codes[:], scales[:])
             for at, a, b, engine in W_AT:
                 if at == o:
                     prepare_w(a, b, engine)
@@ -240,8 +248,8 @@ def tile_attend_deform_kernel(tc, xT, w, part, offs, out):
                         out=acc[:],
                         lhsT=w_codes[:, m_cols].bitcast(FP8X4),
                         lhsT_scale=w_scales[:, m_cols],
-                        rhs=e_codes[q][:].bitcast(FP8X4),
-                        rhs_scale=e_scales[q][:],
+                        rhs=e_codes[q].bitcast(FP8X4),
+                        rhs_scale=e_scales[q],
                         start=(q == 0),
                         stop=(q == O - 1),
                     )

from contextlib import ExitStack

import concourse.mybir as mybir
from concourse.masks import make_identity

O, G, K, T, D, M = 9, 256, 4, 2048, 512, 128
P = 128
PACK = 4
HALVES = G // P
W = D // HALVES

FLOPS = 2 * O * D * M * G
BYTES = 4 * D * T + 4 * O * D * M + 4 * O * G * K + 2 * P * (O * G * K // 16) + 4 * M * G

F32 = mybir.dt.float32
BF16 = mybir.dt.bfloat16
U32 = mybir.dt.uint32
U16 = mybir.dt.uint16
U8 = mybir.dt.uint8
FP8X4 = mybir.dt.float8_e4m3fn_x4
COPY = mybir.ActivationFunctionType.Copy
MULT = mybir.AluOpType.mult
ADD = mybir.AluOpType.add

CHUNKS = ((0, 512), (512, 512), (1024, 512), (1536, 256), (1792, 256))
V_CORNERS = (0, 1, 1, 1, 1, 2, 0, 2, 0)
W_AT = ((1, 0, 4, "G"), (2, 4, 8, "S"), (4, 8, 9, "S"))
MM_AT = (3, 7, 8)
U1_ON_V = (1792,)
V_ADDS = (7,)
TAIL = ("pairs", "chain")
PICK_BUFS = 2
PROD_BUFS = 2
XT = 5
EP = 2
E_GROUPS = ((0, 1, 2, 3), (4, 5, 6, 7), (8,))


def tile_attend_deform_kernel(tc, xT, w, part, offs, out):
    nc = tc.nc
    with ExitStack() as ctx:
        held = ctx.enter_context(tc.tile_pool(name="held", bufs=1))
        duo = ctx.enter_context(tc.tile_pool(name="duo", bufs=2))
        psum = ctx.enter_context(tc.psum_pool(name="psum", bufs=1))

        offsets = held.tile([P, O * G * K // 16], U16)
        ident = held.tile([P, P], F32)
        part_rows = held.tile([P, G * K // HALVES], F32)
        words = [held.tile([P, 2 * T], BF16, name="words%d" % u) for u in range(2)]

        nc.vector.memset(part_rows[:], 0.0)
        make_identity(nc, ident[:])
        nc.scalar.dma_start(
            out=part_rows[0 : O * HALVES, :],
            in_=part[0:1, :].rearrange("a (b e) -> (a b) e", e=G * K // HALVES),
        )

        x_rows = xT.rearrange("(p t) c -> p t c", t=PACK)
        chunk = 0
        for u in range(2):
            for c, wide in CHUNKS:
                x32 = duo.tile([P, 2, wide], F32, name="x32", tag="prod%d" % (chunk % K), bufs=PROD_BUFS)
                chunk += 1
                nc.sync.dma_start(out=x32[:], in_=x_rows[:, 2 * u : 2 * u + 2, c : c + wide])
                dst = words[u][:, 2 * c : 2 * (c + wide)].rearrange("p (c e) -> p c e", e=2)
                src = x32[:].rearrange("p e c -> p c e")
                if u == 0 or c in U1_ON_V:
                    nc.vector.tensor_copy(out=dst, in_=src)
                else:
                    nc.scalar.activation(out=dst, in_=src, func=COPY)
            if u == 0:
                nc.sync.dma_start(offsets[:], offs)

        part_ps = psum.tile([P, 512], F32, tag="xt", bufs=XT)
        for j in range(K):
            nc.tensor.transpose(part_ps[:, j * P : (j + 1) * P], part_rows[:, j::K], ident[:])
        part_col = held.tile([P, K, O * HALVES], F32)
        nc.scalar.activation(
            out=part_col[:],
            in_=part_ps[:].rearrange("p (j b) -> p j b", j=K)[:, :, 0 : O * HALVES],
            func=COPY,
        )

        w_rows = w.rearrange("o (p j) m -> p o j m", j=PACK)
        w_bf = held.tile([P, O * M * PACK], BF16, align_bytes=64)
        w_codes = held.tile([P, O * M], U32, align_bytes=64)
        w_scales = held.tile([P, O * M], U8, align_bytes=64)

        def prepare_w(a, b, engine):
            w32 = held.tile([P, 4, PACK, M], F32, name="first1")
            for o in range(a, b):
                nc.sync.dma_start(out=w32[:, o - a], in_=w_rows[:, o])
            dst = w_bf[:, a * M * PACK : b * M * PACK].rearrange("p (o m j) -> p o m j", o=b - a, j=PACK)
            src = w32[:, 0 : b - a].rearrange("p o j m -> p o m j")
            if engine == "V":
                nc.vector.tensor_copy(out=dst, in_=src)
            elif engine == "G":
                nc.gpsimd.tensor_scalar(out=dst, in0=src, scalar1=1.0, scalar2=0.0, op0=MULT, op1=ADD)
            else:
                nc.scalar.activation(out=dst, in_=src, func=COPY)
            nc.vector.quantize_mx(
                out=w_codes[:, a * M : b * M].bitcast(FP8X4),
                scales=w_scales[:, a * M : b * M],
                in_=w_bf[:, PACK * a * M : PACK * b * M],
            )

        acc = psum.tile([M, G], F32)
        e_codes, e_scales, e_vals, closes = {}, {}, {}, {}
        for group in E_GROUPS:
            n = len(group)
            vals = held.tile([P, n * G * PACK], BF16, name="e_vals%d" % group[0], align_bytes=64)
            codes = held.tile([P, n * G], U32, name="e_codes%d" % group[0], align_bytes=64)
            scales = held.tile([P, n * G], U8, name="e_scales%d" % group[0], align_bytes=64)
            for i in range(n):
                e_vals[group[i]] = vals[:, i * G * PACK : (i + 1) * G * PACK]
                e_codes[group[i]] = codes[:, i * G : (i + 1) * G]
                e_scales[group[i]] = scales[:, i * G : (i + 1) * G]
            closes[group[-1]] = (vals, codes, scales)

        def gather(picked, u, o, a, b):
            cols = slice((o * G * K + a) // 16, (o * G * K + b) // 16)
            nc.vector.tensor_copy(picked[:, a:b], words[u][:].bitcast(U32).indirect(offsets[:, cols]))

        def turn(picked, pieces):
            bank = psum.tile([P, 512], F32, name="bank", tag="xt", bufs=XT)
            for i in range(len(pieces)):
                u, h, j = pieces[i]
                entries = picked[u][:].bitcast(F32)[:, h * P * K + j : (h + 1) * P * K : K]
                nc.tensor.transpose(bank[:, i * P : (i + 1) * P], entries, ident[:])
            return bank[:].bitcast(BF16)

        def scale(o, h, j):
            return part_col[:, j, HALVES * o + h : HALVES * o + h + 1]

        def turn_back(e_rows, halves, e_k):
            e_words = e_rows.bitcast(F32)
            n = len(halves) * P
            e_ps = psum.tile([P, 512], F32, name="e_ps", tag="e_ps", bufs=EP)
            for i in range(len(halves)):
                for u in range(2):
                    nc.tensor.transpose(
                        e_ps[:, u * n + i * P : u * n + (i + 1) * P],
                        e_words[:, (2 * i + u) * P : (2 * i + u + 1) * P],
                        ident[:],
                    )
            nc.scalar.copy(
                out=e_k.bitcast(F32).rearrange("p (g u) -> p g u", u=2),
                in_=e_ps[:, 0 : 2 * n].rearrange("p (u g) -> p g u", u=2),
            )

        def quantise_e(vals, codes, scales):
            nc.vector.quantize_mx(out=codes.bitcast(FP8X4), scales=scales, in_=vals)

        done = 0
        for o in range(O):
            e_k = e_vals[o]
            picked = [duo.tile([P, G * K], U32, name="picked%d" % u, bufs=PICK_BUFS) for u in range(2)]
            if o == 0:
                e_rows = duo.tile([P, HALVES, 2, W], BF16, align_bytes=64)
                for u in range(2):
                    gather(picked[u], u, o, 0, G * K)
                    prods = held.tile([P, K, HALVES * W], F32, name="first%d" % u)
                    for j0 in range(0, K, 2):
                        vals = turn(picked, [(u, h, j) for j in (j0, j0 + 1) for h in range(HALVES)])
                        for i in range(4):
                            j, h = j0 + i // 2, i % 2
                            nc.scalar.activation(
                                out=prods[:, j, h * W : (h + 1) * W], in_=vals[:, i * W : (i + 1) * W],
                                func=COPY, scale=scale(o, h, j),
                            )
                    pairs = held.tile([P, 2, HALVES * W], F32, name="pairs%d" % u)
                    nc.gpsimd.tensor_tensor(out=pairs[:], in0=prods[:, 0:2], in1=prods[:, 2:4], op=ADD)
                    nc.gpsimd.tensor_tensor(
                        out=e_rows[:, :, u], in0=pairs[:, 0].rearrange("p (h w) -> p h w", h=HALVES),
                        in1=pairs[:, 1].rearrange("p (h w) -> p h w", h=HALVES), op=ADD,
                    )
                turn_back(e_rows[:].rearrange("p h u w -> p (h u w)"), (0, 1), e_k)
            elif o < O - 1:
                for u in range(2):
                    gather(picked[u], u, o, 0, G * K)
                prods = []
                for j in range(K):
                    vals = turn(picked, [(u, h, j) for h in range(HALVES) for u in range(2)])
                    prod = duo.tile([P, HALVES * D], F32, name="prod%d" % j, bufs=PROD_BUFS)
                    for h in range(HALVES):
                        part_h = slice(h * D, (h + 1) * D)
                        if j >= K - V_CORNERS[o]:
                            onto = prods[2] if V_CORNERS[o] == 1 else prods[j - 2]
                            nc.vector.scalar_tensor_tensor(
                                out=prod[:, part_h], in0=vals[:, part_h], scalar=scale(o, h, j),
                                in1=onto[:, part_h], op0=MULT, op1=ADD,
                            )
                        else:
                            nc.scalar.activation(
                                out=prod[:, part_h], in_=vals[:, part_h], func=COPY, scale=scale(o, h, j)
                            )
                    prods.append(prod)
                if V_CORNERS[o] == 2:
                    halves = (prods[2], prods[3])
                else:
                    sum01 = duo.tile([P, HALVES * D], F32)
                    nc.gpsimd.tensor_tensor(out=sum01[:], in0=prods[0][:], in1=prods[1][:], op=ADD)
                    halves = (sum01, prods[3])
                    if V_CORNERS[o] == 0:
                        sum23 = duo.tile([P, HALVES * D], F32)
                        nc.gpsimd.tensor_tensor(out=sum23[:], in0=prods[2][:], in1=prods[3][:], op=ADD)
                        halves = (sum01, sum23)
                e_rows = duo.tile([P, HALVES * D], BF16, align_bytes=64)
                adder = nc.vector if o in V_ADDS else nc.gpsimd
                adder.tensor_tensor(out=e_rows[:], in0=halves[0][:], in1=halves[1][:], op=ADD)
                turn_back(e_rows[:], (0, 1), e_k)
            else:
                for h in range(HALVES):
                    for u in range(2):
                        gather(picked[u], u, o, h * P * K, (h + 1) * P * K)
                    kind = TAIL[h]
                    e_rows = duo.tile([P, D], BF16, name="e_last", align_bytes=64)
                    vals = {}
                    for js in ((0,), (1, 2), (3,)) if kind == "chain" else ((0, 1), (2, 3)):
                        bank = turn(picked, [(u, h, j) for j in js for u in range(2)])
                        for i in range(len(js)):
                            vals[js[i]] = bank[:, i * D : (i + 1) * D]
                    prods = held.tile([P, K, D], F32, name="last%d" % h, tag="first%d" % h)
                    on_scalar = {"chain": 1, "pairs": 2}[kind]
                    for j in range(K):
                        if j < on_scalar:
                            nc.scalar.activation(out=prods[:, j], in_=vals[j], func=COPY, scale=scale(o, h, j))
                        else:
                            nc.vector.scalar_tensor_tensor(
                                out=e_rows[:] if kind == "chain" and j == K - 1 else prods[:, j], in0=vals[j],
                                scalar=scale(o, h, j), in1=prods[:, j - on_scalar], op0=MULT, op1=ADD,
                            )
                    if kind == "pairs":
                        nc.vector.tensor_tensor(out=e_rows[:], in0=prods[:, 2], in1=prods[:, 3], op=ADD)
                    turn_back(e_rows[:], (h,), e_k[:, h * P * PACK : (h + 1) * P * PACK])
                    cols = slice(h * P, (h + 1) * P)
                    quantise_e(e_k[:, h * P * PACK : (h + 1) * P * PACK], e_codes[o][:, cols], e_scales[o][:, cols])
            if o in closes and o < O - 1:
                vals, codes, scales = closes[o]
                quantise_e(vals[:], codes[:], scales[:])
            for at, a, b, engine in W_AT:
                if at == o:
                    prepare_w(a, b, engine)
            if o in MM_AT:
                for q in range(done, o + 1):
                    m_cols = slice(q * M, (q + 1) * M)
                    nc.tensor.matmul_mx(
                        out=acc[:],
                        lhsT=w_codes[:, m_cols].bitcast(FP8X4),
                        lhsT_scale=w_scales[:, m_cols],
                        rhs=e_codes[q].bitcast(FP8X4),
                        rhs_scale=e_scales[q],
                        start=(q == 0),
                        stop=(q == O - 1),
                    )
                done = o + 1
        result = held.tile([M, G], F32)
        nc.vector.tensor_copy(out=result[:], in_=acc[:])
        nc.sync.dma_start(out=out, in_=result[:])
